import numpy as np
import ml_dtypes


def mxq(x, axis, fmt="e4m3"):
    dtype, down = {"e4m3": (ml_dtypes.float8_e4m3fn, 7), "e5m2": (ml_dtypes.float8_e5m2, 14)}[fmt]
    v = np.moveaxis(np.asarray(x, np.float32).astype(ml_dtypes.bfloat16).astype(np.float64), axis, -1)
    blocks = v.reshape(v.shape[:-1] + (-1, 32))
    amax = np.abs(blocks).max(-1, keepdims=True)
    byte = np.maximum(np.where(amax > 0, np.frexp(amax)[1] - 1 + 127, 0) - down, 1)
    scale = np.exp2(byte - 127.0)
    codes = (blocks / scale).astype(np.float32).astype(dtype).astype(np.float64)
    return np.moveaxis((codes * scale).reshape(v.shape), -1, axis)


WIDE = False


def mx_kscale(k):
    if not WIDE:
        return np.ones(k)
    levels = np.array([30, -30])
    if k % 512:
        return np.exp2(np.random.permutation(np.resize(levels, k // 32))).repeat(32)
    a = np.empty((k // 512, 16))
    for p in range(k // 512):
        a[p, :8] = np.random.permutation(np.resize(levels, 8))
        for g in range(8):
            far = levels[np.abs(levels - a[p, g]) >= 10]
            a[p, g + 8] = far[np.random.randint(len(far))]
    return np.exp2(a.ravel()).repeat(32)


def f64(x):
    return np.asarray(x).astype(np.float64)


def striped(idx):
    return np.tile(np.asarray(idx).reshape(-1, 16).T, (8, 1)).astype(np.uint16)


def unstriped(offs):
    return offs[:16].T.reshape(-1).astype(np.int64)


E2M1 = np.array([0.0, 0.5, 1.0, 1.5, 2.0, 3.0, 4.0, 6.0, -0.0, -0.5, -1.0, -1.5, -2.0, -3.0, -4.0, -6.0])


def pack_weight(w, fmt):
    k, n = w.shape
    w = f64(np.asarray(w, np.float32).astype(ml_dtypes.bfloat16)).reshape(k // 32, 32, n)
    amax = np.abs(w).max(1)
    if fmt == "e4m3":
        byte = np.frexp(amax)[1] - 1 + 127 - 7
    else:
        mant, ex = np.frexp(amax / 6.0)
        byte = np.where(mant > 0.5, ex, ex - 1) + 127
    byte = np.clip(np.where(amax > 0, byte, 1), 1, 254)
    scaled = (w * np.exp2(127.0 - byte)[:, None, :]).reshape(k, n).astype(np.float32)
    by_word = np.ascontiguousarray(scaled.reshape(k // 512, 128, 4, n).transpose(0, 1, 3, 2))
    if fmt == "e4m3":
        words = by_word.astype(ml_dtypes.float8_e4m3fn).view(np.uint8)
    else:
        c = by_word.astype(ml_dtypes.float4_e2m1fn).view(np.uint8) & 0xF
        words = (c[..., 0::2] | (c[..., 1::2] << 4)).reshape(k // 512, 128, 2 * n)
    return np.ascontiguousarray(words), np.ascontiguousarray(byte.astype(np.uint8).reshape(k // 512, 16, n))


def unpack_weight(words, scales, fmt):
    g, _, n = scales.shape
    words = np.ascontiguousarray(words).reshape(g, 128, n, -1)
    if fmt == "e4m3":
        vals = words.view(ml_dtypes.float8_e4m3fn).astype(np.float64)
    else:
        nib = np.empty((g, 128, n, 4), np.uint8)
        nib[..., 0::2] = words & 0xF
        nib[..., 1::2] = words >> 4
        vals = E2M1[nib]
    vals = vals * np.repeat(np.exp2(scales.astype(np.float64) - 127.0), 8, axis=1)[..., None]
    return vals.transpose(0, 1, 3, 2).reshape(g * 512, n)


K, F, T, Z, J, R, V, I, N, S, E = 512, 512, 1024, 1024, 256, 512, 1024, 512, 256, 1024, 1024


def setup_inputs():
    n = np.random.standard_normal
    idx = np.random.permutation(T)[:J]
    idx2 = np.random.permutation(Z)[:J]
    idx3 = np.random.permutation(V)[:I]
    idx4 = np.random.permutation(I)[:J]
    idx5 = np.random.permutation(S)[:N]
    idx6 = np.random.permutation(E)[:J]
    fk = mx_kscale(K)
    fr = mx_kscale(R)
    ff = mx_kscale(F)
    xtp = pack_weight(n((K, T)) / fk[:, None], "e2m1")
    wp = pack_weight(n((K, R)) * 1 / np.sqrt(K) * fk[:, None] * fr, "e4m3")
    xop = pack_weight(n((F, Z)) / ff[:, None], "e4m3")
    w0p = pack_weight(n((F, R)) * 1 / np.sqrt(F) * ff[:, None] * fr, "e2m1")
    vsp = pack_weight(n((R, S)) * 1 / np.sqrt(R) / fr[:, None], "e2m1")
    return {
        "xt_words": xtp[0],
        "xt_scales": xtp[1],
        "w_words": wp[0],
        "w_scales": wp[1],
        "xo_words": xop[0],
        "xo_scales": xop[1],
        "w0_words": w0p[0],
        "w0_scales": w0p[1],
        "tb": (n((R, V)) * 0.8 * fr[:, None]).astype(np.float32),
        "vs_words": vsp[0],
        "vs_scales": vsp[1],
        "offs": striped(idx),
        "offs2": striped(idx2),
        "offs3": striped(idx3),
        "offs4": striped(idx4),
        "offs5": striped(idx5),
        "offs6": striped(idx6),
    }


def reference(xt_words, xt_scales, w_words, w_scales, xo_words, xo_scales, w0_words, w0_scales, tb, vs_words, vs_scales, offs, offs2, offs3, offs4, offs5, offs6):
    idx = unstriped(offs)
    idx2 = unstriped(offs2)
    idx3 = unstriped(offs3)
    idx4 = unstriped(offs4)
    idx5 = unstriped(offs5)
    idx6 = unstriped(offs6)
    xtu = unpack_weight(xt_words, xt_scales, "e2m1")
    wu = unpack_weight(w_words, w_scales, "e4m3")
    xou = unpack_weight(xo_words, xo_scales, "e4m3")
    w0u = unpack_weight(w0_words, w0_scales, "e2m1")
    vsu = unpack_weight(vs_words, vs_scales, "e2m1")
    xtidxg = xtu[:, idx]
    xoidx2g = xou[:, idx2]
    a = wu.T @ xtidxg + w0u.T @ xoidx2g
    ts = f64(tb)[:, idx3]
    hid = np.maximum(a, ts[:, idx4])
    vsidx5g = vsu[:, idx5]
    hidq = mxq(hid, 0, "e5m2")
    p = vsidx5g.T @ hidq
    y = np.zeros((N, E))
    y[:, idx6] = p
    return y

@@ -1,0 +1,187 @@
+from contextlib import ExitStack
+
+import concourse.mybir as mybir
+from concourse.masks import make_identity
+
+K, F, T, Z, J, R, V, I, N, S, E = 512, 512, 1024, 1024, 256, 512, 1024, 512, 256, 1024, 1024
+FLOPS = 2 * K * R * J + 2 * F * R * J + 2 * R * N * J
+
+F32 = mybir.dt.float32
+BF16 = mybir.dt.bfloat16
+I32 = mybir.dt.int32
+U32 = mybir.dt.uint32
+U16 = mybir.dt.uint16
+U8 = mybir.dt.uint8
+E4M3X4 = mybir.dt.float8_e4m3fn_x4
+E5M2X4 = mybir.dt.float8_e5m2_x4
+E2M1X4 = mybir.dt.float4_e2m1fn_x4
+COPY = mybir.ActivationFunctionType.Copy
+MAX = mybir.AluOpType.max
+
+P = 128
+PACK = 4
+GROUP = 16
+HALVES = J // P
+
+
+def tile_list_tabletwice_bank_store_scattered_kernel(
+    tc, xt_words, xt_scales, w_words, w_scales, xo_words, xo_scales, w0_words, w0_scales, tb,
+    vs_words, vs_scales, offs, offs2, offs3, offs4, offs5, offs6, out,
+):
+    nc = tc.nc
+    with ExitStack() as ctx:
+        lists = ctx.enter_context(tc.tile_pool(name="lists", bufs=1))
+        sb = ctx.enter_context(tc.tile_pool(name="sb", bufs=1))
+        psum = ctx.enter_context(tc.psum_pool(name="psum", bufs=1))
+
+        def new_tile(shape, dtype, name):
+            return sb.tile(shape, dtype, name=name, align_bytes=64)
+
+        def load_list(src, name):
+            dst = lists.tile(list(src.shape), U16, name=name)
+            nc.sync.dma_start(dst[:], src)
+            return dst
+
+        def load_words(src, columns, dtype, name):
+            dst = new_tile([P, columns], dtype, name)
+            nc.sync.dma_start(out=dst[:].bitcast(I32), in_=src.bitcast(I32))
+            return dst
+
+        def zeroed_plane(engine, columns, name):
+            plane = new_tile([P, columns], U8, name)
+            engine.memset(plane[:].bitcast(I32), 0)
+            return plane
+
+        def load_plane(queue, plane, src, quadrants):
+            for q in quadrants:
+                queue.dma_start(
+                    out=plane[32 * q : 32 * q + 4, :].bitcast(I32),
+                    in_=src[0, 4 * q : 4 * q + 4, :].bitcast(I32),
+                )
+
+        def load_level_rows(t):
+            dst = new_tile([P, V], F32, f"tb{t}")
+            nc.sync.dma_start(out=dst[:], in_=tb.rearrange("(p t) v -> p t v", t=PACK)[:, t, :])
+            return dst
+
+        def gather_packed(window, offsets, dtype, name):
+            dst = new_tile([P, J], dtype, name)
+            nc.vector.tensor_copy(dst[:], window[:].indirect(offsets[:]))
+            return dst
+
+        def gather_f32(on_scalar, dst, window, offsets):
+            if on_scalar:
+                nc.scalar.activation(dst, window[:].indirect(offsets), COPY)
+            else:
+                nc.vector.tensor_copy(dst, window[:].indirect(offsets))
+
+        xt_plane = zeroed_plane(nc.vector, T, "xt_plane")
+        xo_plane = zeroed_plane(nc.vector, Z, "xo_plane")
+        w_plane = zeroed_plane(nc.vector, R, "w_plane")
+        w0_plane = zeroed_plane(nc.vector, R, "w0_plane")
+        vs_plane = zeroed_plane(nc.gpsimd, S, "vs_plane")
+        load_plane(nc.gpsimd, vs_plane, vs_scales, (0, 1, 2, 3))
+        identity = new_tile([P, P], F32, "identity")
+        make_identity(nc, identity[:])
+        pages = [new_tile([P, E], F32, f"page{u}") for u in range(N // P)]
+        for page in pages:
+            nc.vector.memset(page[:], 0.0)
+
+        idx3 = load_list(offs3, "idx3")
+        tbs = [load_level_rows(0)]
+        idx = load_list(offs, "idx")
+        xt_w = load_words(xt_words[0], T, U16, "xt_w")
+        idx4 = load_list(offs4, "idx4")
+        load_plane(nc.sync, xt_plane, xt_scales, (0, 1))
+        xo_w = load_words(xo_words[0].rearrange("p c r -> p (c r)"), Z, U32, "xo_w")
+        load_plane(nc.sync, xt_plane, xt_scales, (2, 3))
+        w_w = load_words(w_words[0].rearrange("p c r -> p (c r)"), R, U32, "w_w")
+        idx2 = load_list(offs2, "idx2")
+        load_plane(nc.sync, xo_plane, xo_scales, (0,))
+        tbs.append(load_level_rows(1))
+        load_plane(nc.sync, xo_plane, xo_scales, (1, 2, 3))
+        w0_w = load_words(w0_words[0], R, U16, "w0_w")
+        load_plane(nc.sync, w_plane, w_scales, (0, 1))
+        tbs.append(load_level_rows(2))
+        load_plane(nc.sync, w_plane, w_scales, (2, 3))
+        load_plane(nc.sync, w0_plane, w0_scales, (0, 1, 2, 3))
+        tbs.append(load_level_rows(3))
+        idx5 = load_list(offs5, "idx5")
+        vs_w = load_words(vs_words[0], S, U16, "vs_w")
+        idx6 = load_list(offs6, "idx6")
+
+        short = [new_tile([P, I], F32, f"short{t}") for t in range(PACK)]
+        level = [new_tile([P, PACK, P], F32, f"level{h}") for h in range(HALVES)]
+        half_list = I // 2 // GROUP
+        cols = P // GROUP
+
+        def shorten(t, part, on_scalar):
+            gather_f32(on_scalar, short[t][:, part * (I // 2) : (part + 1) * (I // 2)], tbs[t],
+                       idx3[:, part * half_list : (part + 1) * half_list])
+
+        def look_up(t, h, on_scalar):
+            gather_f32(on_scalar, level[h][:, t, :], short[t], idx4[:, h * cols : (h + 1) * cols])
+
+        shorten(0, 0, True)
+        shorten(0, 1, False)
+        xt_g = gather_packed(xt_w, idx, U16, "xt_g")
+        look_up(0, 0, True)
+        look_up(0, 1, True)
+        xt_gs = gather_packed(xt_plane, idx, U8, "xt_gs")
+        xo_g = gather_packed(xo_w, idx2, U32, "xo_g")
+        gather_f32(True, short[1][:], tbs[1], idx3[:])
+        xo_gs = gather_packed(xo_plane, idx2, U8, "xo_gs")
+        look_up(1, 0, False)
+        look_up(1, 1, False)
+        shorten(2, 0, True)
+        shorten(2, 1, False)
+        look_up(2, 0, False)
+        look_up(2, 1, False)
+
+        a_slot = [psum.tile([P, R], F32, name=f"a_slot{h}") for h in range(HALVES)]
+        a_row = [psum.tile([P, PACK, P], F32, name=f"a_row{h}") for h in range(HALVES)]
+        for h in range(HALVES):
+            js = slice(h * P, (h + 1) * P)
+            nc.tensor.matmul_mx(out=a_slot[h][:], lhsT=xt_g[:, js].bitcast(E2M1X4), lhsT_scale=xt_gs[:, js],
+                                rhs=w_w[:].bitcast(E4M3X4), rhs_scale=w_plane[:], start=True, stop=False)
+            nc.tensor.matmul_mx(out=a_slot[h][:], lhsT=xo_g[:, js].bitcast(E4M3X4), lhsT_scale=xo_gs[:, js],
+                                rhs=w0_w[:].bitcast(E2M1X4), rhs_scale=w0_plane[:], start=False, stop=True)
+
+        def turn(h):
+            dealt = new_tile([P, PACK, P], F32, f"dealt{h}")
+            nc.scalar.copy(dealt[:], a_slot[h][:].rearrange("j (m t) -> j t m", t=PACK))
+            for t in range(PACK):
+                nc.tensor.transpose(a_row[h][:, t, :], dealt[:, t, :], identity[:])
+
+        turn(0)
+        shorten(3, 0, True)
+        shorten(3, 1, False)
+        look_up(3, 0, True)
+        turn(1)
+        look_up(3, 1, True)
+        vs_gs = gather_packed(vs_plane, idx5, U8, "vs_gs")
+        vs_g = gather_packed(vs_w, idx5, U16, "vs_g")
+
+        results = []
+        for h in range(HALVES):
+            hid = new_tile([P, P, PACK], BF16, "hid")
+            nc.vector.tensor_tensor(hid[:].rearrange("p (c i) t -> p c t i", i=PACK),
+                                    a_row[h][:].rearrange("p t (c i) -> p c t i", i=PACK),
+                                    level[h][:].rearrange("p t (c i) -> p c t i", i=PACK), MAX)
+            codes = new_tile([P, P], U32, f"codes{h}")
+            scales = new_tile([P, P], U8, f"scales{h}")
+            nc.vector.quantize_mx(out=codes[:].bitcast(E5M2X4), scales=scales[:],
+                                  in_=hid[:].rearrange("p j t -> p (j t)"))
+            p_bank = psum.tile([P, N // P, P], F32, name=f"p_bank{h}")
+            for u in range(N // P):
+                ns = slice(u * P, (u + 1) * P)
+                nc.tensor.matmul_mx(out=p_bank[:, u, :], lhsT=vs_g[:, ns].bitcast(E2M1X4), lhsT_scale=vs_gs[:, ns],
+                                    rhs=codes[:].bitcast(E5M2X4), rhs_scale=scales[:], start=True, stop=True)
+            result = new_tile([P, N // P, P], F32, f"result{h}")
+            nc.scalar.copy(result[:], p_bank[:])
+            nc.scalar.activation(pages[0][:].indirect(idx6[:, h * cols : (h + 1) * cols]), result[:, 0, :], COPY)
+            results.append(result)
+        for h in range(HALVES):
+            nc.vector.tensor_copy(pages[1][:].indirect(idx6[:, h * cols : (h + 1) * cols]), results[h][:, 1, :])
+        for u in range(N // P):
+            nc.sync.dma_start(out=out[u * P : (u + 1) * P, :], in_=pages[u][:])

@@ -78,8 +78,9 @@ def tile_list_tabletwice_bank_store_scattered_kernel(
         xt_plane = zeroed_plane(nc.vector, T, "xt_plane")
         xo_plane = zeroed_plane(nc.vector, Z, "xo_plane")
         w_plane = zeroed_plane(nc.vector, R, "w_plane")
-        w0_plane = zeroed_plane(nc.vector, R, "w0_plane")
+        w0_plane = zeroed_plane(nc.gpsimd, R, "w0_plane")
         vs_plane = zeroed_plane(nc.gpsimd, S, "vs_plane")
+        load_plane(nc.gpsimd, w0_plane, w0_scales, (0, 1, 2, 3))
         load_plane(nc.gpsimd, vs_plane, vs_scales, (0, 1, 2, 3))
         identity = new_tile([P, P], F32, "identity")
         make_identity(nc, identity[:])
@@ -95,93 +96,116 @@ def tile_list_tabletwice_bank_store_scattered_kernel(
         load_plane(nc.sync, xt_plane, xt_scales, (0, 1))
         xo_w = load_words(xo_words[0].rearrange("p c r -> p (c r)"), Z, U32, "xo_w")
         load_plane(nc.sync, xt_plane, xt_scales, (2, 3))
-        w_w = load_words(w_words[0].rearrange("p c r -> p (c r)"), R, U32, "w_w")
+        tbs.append(load_level_rows(1))
         idx2 = load_list(offs2, "idx2")
         load_plane(nc.sync, xo_plane, xo_scales, (0,))
-        tbs.append(load_level_rows(1))
-        load_plane(nc.sync, xo_plane, xo_scales, (1, 2, 3))
         w0_w = load_words(w0_words[0], R, U16, "w0_w")
-        load_plane(nc.sync, w_plane, w_scales, (0, 1))
+        load_plane(nc.sync, xo_plane, xo_scales, (1, 2, 3))
         tbs.append(load_level_rows(2))
+        load_plane(nc.sync, w_plane, w_scales, (0, 1))
+        w_w = load_words(w_words[0].rearrange("p c r -> p (c r)"), R, U32, "w_w")
         load_plane(nc.sync, w_plane, w_scales, (2, 3))
-        load_plane(nc.sync, w0_plane, w0_scales, (0, 1, 2, 3))
-        tbs.append(load_level_rows(3))
         idx5 = load_list(offs5, "idx5")
+        tbs.append(load_level_rows(3))
         vs_w = load_words(vs_words[0], S, U16, "vs_w")
         idx6 = load_list(offs6, "idx6")
 
         short = [new_tile([P, I], F32, f"short{t}") for t in range(PACK)]
         level = [new_tile([P, PACK, P], F32, f"level{h}") for h in range(HALVES)]
-        half_list = I // 2 // GROUP
         cols = P // GROUP
 
-        def shorten(t, part, on_scalar):
-            gather_f32(on_scalar, short[t][:, part * (I // 2) : (part + 1) * (I // 2)], tbs[t],
-                       idx3[:, part * half_list : (part + 1) * half_list])
+        def shorten(t, scalar_entries):
+            cut = scalar_entries // GROUP
+            gather_f32(True, short[t][:, :scalar_entries], tbs[t], idx3[:, :cut])
+            gather_f32(False, short[t][:, scalar_entries:], tbs[t], idx3[:, cut:])
 
         def look_up(t, h, on_scalar):
             gather_f32(on_scalar, level[h][:, t, :], short[t], idx4[:, h * cols : (h + 1) * cols])
 
-        shorten(0, 0, True)
-        shorten(0, 1, False)
+        shorten(0, I // 2)
         xt_g = gather_packed(xt_w, idx, U16, "xt_g")
         look_up(0, 0, True)
         look_up(0, 1, True)
         xt_gs = gather_packed(xt_plane, idx, U8, "xt_gs")
-        xo_g = gather_packed(xo_w, idx2, U32, "xo_g")
         gather_f32(True, short[1][:], tbs[1], idx3[:])
+        look_up(1, 0, True)
+        look_up(1, 1, True)
+        xo_g = gather_packed(xo_w, idx2, U32, "xo_g")
         xo_gs = gather_packed(xo_plane, idx2, U8, "xo_gs")
-        look_up(1, 0, False)
-        look_up(1, 1, False)
-        shorten(2, 0, True)
-        shorten(2, 1, False)
+        shorten(2, I // 2)
         look_up(2, 0, False)
-        look_up(2, 1, False)
+        look_up(2, 1, True)
+        vs_gs = gather_packed(vs_plane, idx5, U8, "vs_gs")
 
         a_slot = [psum.tile([P, R], F32, name=f"a_slot{h}") for h in range(HALVES)]
         a_row = [psum.tile([P, PACK, P], F32, name=f"a_row{h}") for h in range(HALVES)]
-        for h in range(HALVES):
+        def notes_pass(h, first):
+            js = slice(h * P, (h + 1) * P)
+            nc.tensor.matmul_mx(out=a_slot[h][:], lhsT=xo_g[:, js].bitcast(E4M3X4), lhsT_scale=xo_gs[:, js],
+                                rhs=w0_w[:].bitcast(E2M1X4), rhs_scale=w0_plane[:], start=first, stop=not first)
+
+        def tokens_pass(h, first):
             js = slice(h * P, (h + 1) * P)
             nc.tensor.matmul_mx(out=a_slot[h][:], lhsT=xt_g[:, js].bitcast(E2M1X4), lhsT_scale=xt_gs[:, js],
-                                rhs=w_w[:].bitcast(E4M3X4), rhs_scale=w_plane[:], start=True, stop=False)
-            nc.tensor.matmul_mx(out=a_slot[h][:], lhsT=xo_g[:, js].bitcast(E4M3X4), lhsT_scale=xo_gs[:, js],
-                                rhs=w0_w[:].bitcast(E2M1X4), rhs_scale=w0_plane[:], start=False, stop=True)
+                                rhs=w_w[:].bitcast(E4M3X4), rhs_scale=w_plane[:], start=first, stop=not first)
 
-        def turn(h):
-            dealt = new_tile([P, PACK, P], F32, f"dealt{h}")
+        notes_pass(0, True)
+        tokens_pass(0, False)
+        tokens_pass(1, True)
+        notes_pass(1, False)
+
+        def turn(h, name):
+            dealt = new_tile([P, PACK, P], F32, name)
             nc.scalar.copy(dealt[:], a_slot[h][:].rearrange("j (m t) -> j t m", t=PACK))
             for t in range(PACK):
                 nc.tensor.transpose(a_row[h][:, t, :], dealt[:, t, :], identity[:])
 
-        turn(0)
-        shorten(3, 0, True)
-        shorten(3, 1, False)
+        turn(0, "dealt")
+        shorten(3, 224)
         look_up(3, 0, True)
-        turn(1)
+        turn(1, "tb3")
         look_up(3, 1, True)
-        vs_gs = gather_packed(vs_plane, idx5, U8, "vs_gs")
         vs_g = gather_packed(vs_w, idx5, U16, "vs_g")
 
-        results = []
-        for h in range(HALVES):
-            hid = new_tile([P, P, PACK], BF16, "hid")
+        def larger(h):
+            hid = new_tile([P, P, PACK], BF16, "vs_w")
             nc.vector.tensor_tensor(hid[:].rearrange("p (c i) t -> p c t i", i=PACK),
                                     a_row[h][:].rearrange("p t (c i) -> p c t i", i=PACK),
                                     level[h][:].rearrange("p t (c i) -> p c t i", i=PACK), MAX)
+            return hid
+
+        def quantise(h, hid):
             codes = new_tile([P, P], U32, f"codes{h}")
             scales = new_tile([P, P], U8, f"scales{h}")
             nc.vector.quantize_mx(out=codes[:].bitcast(E5M2X4), scales=scales[:],
                                   in_=hid[:].rearrange("p j t -> p (j t)"))
-            p_bank = psum.tile([P, N // P, P], F32, name=f"p_bank{h}")
+            return codes, scales
+
+        def multiply(dst, u, codes, scales):
+            ns = slice(u * P, (u + 1) * P)
+            nc.tensor.matmul_mx(out=dst, lhsT=vs_g[:, ns].bitcast(E2M1X4), lhsT_scale=vs_gs[:, ns],
+                                rhs=codes[:].bitcast(E5M2X4), rhs_scale=scales[:], start=True, stop=True)
+
+        def page_columns(u, h):
+            return pages[u][:].indirect(idx6[:, h * cols : (h + 1) * cols])
+
+        banks = [[psum.tile([P, P], F32, name=f"bank{h}{u}") for u in range(N // P)] for h in range(HALVES)]
+        results = [[new_tile([P, P], F32, f"result{h}{u}") for u in range(N // P)] for h in range(HALVES)]
+
+        def products(h, hid):
+            codes, scales = quantise(h, hid)
             for u in range(N // P):
-                ns = slice(u * P, (u + 1) * P)
-                nc.tensor.matmul_mx(out=p_bank[:, u, :], lhsT=vs_g[:, ns].bitcast(E2M1X4), lhsT_scale=vs_gs[:, ns],
-                                    rhs=codes[:].bitcast(E5M2X4), rhs_scale=scales[:], start=True, stop=True)
-            result = new_tile([P, N // P, P], F32, f"result{h}")
-            nc.scalar.copy(result[:], p_bank[:])
-            nc.scalar.activation(pages[0][:].indirect(idx6[:, h * cols : (h + 1) * cols]), result[:, 0, :], COPY)
-            results.append(result)
-        for h in range(HALVES):
-            nc.vector.tensor_copy(pages[1][:].indirect(idx6[:, h * cols : (h + 1) * cols]), results[h][:, 1, :])
+                multiply(banks[h][u][:], u, codes, scales)
+            nc.scalar.copy(results[h][0][:], banks[h][0][:])
+            nc.scalar.activation(page_columns(0, h), results[h][0][:], COPY)
+            return codes
+
+        codes = products(0, larger(0))
+        hid = larger(1)
+        nc.vector.tensor_copy(results[0][1][:], banks[0][1][:])
+        products(1, hid)
+        nc.vector.tensor_copy(page_columns(1, 0), results[0][1][:])
+        nc.vector.tensor_copy(results[1][1][:], banks[1][1][:])
+        nc.vector.tensor_copy(page_columns(1, 1), results[1][1][:])
         for u in range(N // P):
             nc.sync.dma_start(out=out[u * P : (u + 1) * P, :], in_=pages[u][:])

@@ -78,10 +78,9 @@ def tile_list_tabletwice_bank_store_scattered_kernel(
         xt_plane = zeroed_plane(nc.vector, T, "xt_plane")
         xo_plane = zeroed_plane(nc.vector, Z, "xo_plane")
         w_plane = zeroed_plane(nc.vector, R, "w_plane")
+        vs_plane = zeroed_plane(nc.vector, S, "vs_plane")
         w0_plane = zeroed_plane(nc.gpsimd, R, "w0_plane")
-        vs_plane = zeroed_plane(nc.gpsimd, S, "vs_plane")
         load_plane(nc.gpsimd, w0_plane, w0_scales, (0, 1, 2, 3))
-        load_plane(nc.gpsimd, vs_plane, vs_scales, (0, 1, 2, 3))
         identity = new_tile([P, P], F32, "identity")
         make_identity(nc, identity[:])
         pages = [new_tile([P, E], F32, f"page{u}") for u in range(N // P)]
@@ -92,22 +91,20 @@ def tile_list_tabletwice_bank_store_scattered_kernel(
         tbs = [load_level_rows(0)]
         idx = load_list(offs, "idx")
         xt_w = load_words(xt_words[0], T, U16, "xt_w")
-        idx4 = load_list(offs4, "idx4")
-        load_plane(nc.sync, xt_plane, xt_scales, (0, 1))
+        load_plane(nc.sync, xt_plane, xt_scales, (0, 1, 2, 3))
         xo_w = load_words(xo_words[0].rearrange("p c r -> p (c r)"), Z, U32, "xo_w")
-        load_plane(nc.sync, xt_plane, xt_scales, (2, 3))
+        idx4 = load_list(offs4, "idx4")
         tbs.append(load_level_rows(1))
         idx2 = load_list(offs2, "idx2")
-        load_plane(nc.sync, xo_plane, xo_scales, (0,))
         w0_w = load_words(w0_words[0], R, U16, "w0_w")
-        load_plane(nc.sync, xo_plane, xo_scales, (1, 2, 3))
+        load_plane(nc.sync, xo_plane, xo_scales, (0, 1, 2, 3))
         tbs.append(load_level_rows(2))
-        load_plane(nc.sync, w_plane, w_scales, (0, 1))
         w_w = load_words(w_words[0].rearrange("p c r -> p (c r)"), R, U32, "w_w")
-        load_plane(nc.sync, w_plane, w_scales, (2, 3))
-        idx5 = load_list(offs5, "idx5")
+        load_plane(nc.sync, w_plane, w_scales, (0, 1, 2, 3))
         tbs.append(load_level_rows(3))
+        idx5 = load_list(offs5, "idx5")
         vs_w = load_words(vs_words[0], S, U16, "vs_w")
+        load_plane(nc.sync, vs_plane, vs_scales, (0, 1, 2, 3))
         idx6 = load_list(offs6, "idx6")
 
         short = [new_tile([P, I], F32, f"short{t}") for t in range(PACK)]
@@ -124,9 +121,9 @@ def tile_list_tabletwice_bank_store_scattered_kernel(
 
         shorten(0, I // 2)
         xt_g = gather_packed(xt_w, idx, U16, "xt_g")
+        xt_gs = gather_packed(xt_plane, idx, U8, "xt_gs")
         look_up(0, 0, True)
         look_up(0, 1, True)
-        xt_gs = gather_packed(xt_plane, idx, U8, "xt_gs")
         gather_f32(True, short[1][:], tbs[1], idx3[:])
         look_up(1, 0, True)
         look_up(1, 1, True)
@@ -135,7 +132,6 @@ def tile_list_tabletwice_bank_store_scattered_kernel(
         shorten(2, I // 2)
         look_up(2, 0, False)
         look_up(2, 1, True)
-        vs_gs = gather_packed(vs_plane, idx5, U8, "vs_gs")
 
         a_slot = [psum.tile([P, R], F32, name=f"a_slot{h}") for h in range(HALVES)]
         a_row = [psum.tile([P, PACK, P], F32, name=f"a_row{h}") for h in range(HALVES)]
@@ -161,14 +157,15 @@ def tile_list_tabletwice_bank_store_scattered_kernel(
                 nc.tensor.transpose(a_row[h][:, t, :], dealt[:, t, :], identity[:])
 
         turn(0, "dealt")
-        shorten(3, 224)
+        shorten(3, I // 2)
         look_up(3, 0, True)
         turn(1, "tb3")
         look_up(3, 1, True)
         vs_g = gather_packed(vs_w, idx5, U16, "vs_g")
+        vs_gs = gather_packed(vs_plane, idx5, U8, "vs_gs")
 
         def larger(h):
-            hid = new_tile([P, P, PACK], BF16, "vs_w")
+            hid = new_tile([P, P, PACK], BF16, "vs_plane")
             nc.vector.tensor_tensor(hid[:].rearrange("p (c i) t -> p c t i", i=PACK),
                                     a_row[h][:].rearrange("p t (c i) -> p c t i", i=PACK),
                                     level[h][:].rearrange("p t (c i) -> p c t i", i=PACK), MAX)
@@ -207,5 +204,5 @@ def tile_list_tabletwice_bank_store_scattered_kernel(
         nc.vector.tensor_copy(page_columns(1, 0), results[0][1][:])
         nc.vector.tensor_copy(results[1][1][:], banks[1][1][:])
         nc.vector.tensor_copy(page_columns(1, 1), results[1][1][:])
-        for u in range(N // P):
-            nc.sync.dma_start(out=out[u * P : (u + 1) * P, :], in_=pages[u][:])
+        nc.scalar.dma_start(out=out[:P, :], in_=pages[0][:])
+        nc.sync.dma_start(out=out[P:, :], in_=pages[1][:])

from contextlib import ExitStack

import concourse.mybir as mybir
from concourse.masks import make_identity

K, F, T, Z, J, R, V, I, N, S, E = 512, 512, 1024, 1024, 256, 512, 1024, 512, 256, 1024, 1024
FLOPS = 2 * K * R * J + 2 * F * R * J + 2 * R * N * J

F32 = mybir.dt.float32
BF16 = mybir.dt.bfloat16
I32 = mybir.dt.int32
U32 = mybir.dt.uint32
U16 = mybir.dt.uint16
U8 = mybir.dt.uint8
E4M3X4 = mybir.dt.float8_e4m3fn_x4
E5M2X4 = mybir.dt.float8_e5m2_x4
E2M1X4 = mybir.dt.float4_e2m1fn_x4
COPY = mybir.ActivationFunctionType.Copy
MAX = mybir.AluOpType.max

P = 128
PACK = 4
GROUP = 16
HALVES = J // P


def tile_list_tabletwice_bank_store_scattered_kernel(
    tc, xt_words, xt_scales, w_words, w_scales, xo_words, xo_scales, w0_words, w0_scales, tb,
    vs_words, vs_scales, offs, offs2, offs3, offs4, offs5, offs6, out,
):
    nc = tc.nc
    with ExitStack() as ctx:
        lists = ctx.enter_context(tc.tile_pool(name="lists", bufs=1))
        sb = ctx.enter_context(tc.tile_pool(name="sb", bufs=1))
        psum = ctx.enter_context(tc.psum_pool(name="psum", bufs=1))

        def new_tile(shape, dtype, name):
            return sb.tile(shape, dtype, name=name, align_bytes=64)

        def load_list(src, name):
            dst = lists.tile(list(src.shape), U16, name=name)
            nc.sync.dma_start(dst[:], src)
            return dst

        def load_words(src, columns, dtype, name):
            dst = new_tile([P, columns], dtype, name)
            nc.sync.dma_start(out=dst[:].bitcast(I32), in_=src.bitcast(I32))
            return dst

        def zeroed_plane(engine, columns, name):
            plane = new_tile([P, columns], U8, name)
            engine.memset(plane[:].bitcast(I32), 0)
            return plane

        def load_plane(queue, plane, src, quadrants):
            for q in quadrants:
                queue.dma_start(
                    out=plane[32 * q : 32 * q + 4, :].bitcast(I32),
                    in_=src[0, 4 * q : 4 * q + 4, :].bitcast(I32),
                )

        def load_level_rows(t):
            dst = new_tile([P, V], F32, f"tb{t}")
            nc.sync.dma_start(out=dst[:], in_=tb.rearrange("(p t) v -> p t v", t=PACK)[:, t, :])
            return dst

        def gather_packed(window, offsets, dtype, name):
            dst = new_tile([P, J], dtype, name)
            nc.vector.tensor_copy(dst[:], window[:].indirect(offsets[:]))
            return dst

        def gather_f32(on_scalar, dst, window, offsets):
            if on_scalar:
                nc.scalar.activation(dst, window[:].indirect(offsets), COPY)
            else:
                nc.vector.tensor_copy(dst, window[:].indirect(offsets))

        xt_plane = zeroed_plane(nc.vector, T, "xt_plane")
        xo_plane = zeroed_plane(nc.vector, Z, "xo_plane")
        w_plane = zeroed_plane(nc.vector, R, "w_plane")
        vs_plane = zeroed_plane(nc.vector, S, "vs_plane")
        w0_plane = zeroed_plane(nc.gpsimd, R, "w0_plane")
        load_plane(nc.gpsimd, w0_plane, w0_scales, (0, 1, 2, 3))
        identity = new_tile([P, P], F32, "identity")
        make_identity(nc, identity[:])
        pages = [new_tile([P, E], F32, f"page{u}") for u in range(N // P)]
        for page in pages:
            nc.vector.memset(page[:], 0.0)

        idx3 = load_list(offs3, "idx3")
        tbs = [load_level_rows(0)]
        idx = load_list(offs, "idx")
        xt_w = load_words(xt_words[0], T, U16, "xt_w")
        load_plane(nc.sync, xt_plane, xt_scales, (0, 1, 2, 3))
        xo_w = load_words(xo_words[0].rearrange("p c r -> p (c r)"), Z, U32, "xo_w")
        idx4 = load_list(offs4, "idx4")
        tbs.append(load_level_rows(1))
        idx2 = load_list(offs2, "idx2")
        w0_w = load_words(w0_words[0], R, U16, "w0_w")
        load_plane(nc.sync, xo_plane, xo_scales, (0, 1, 2, 3))
        tbs.append(load_level_rows(2))
        w_w = load_words(w_words[0].rearrange("p c r -> p (c r)"), R, U32, "w_w")
        load_plane(nc.sync, w_plane, w_scales, (0, 1, 2, 3))
        tbs.append(load_level_rows(3))
        idx5 = load_list(offs5, "idx5")
        vs_w = load_words(vs_words[0], S, U16, "vs_w")
        load_plane(nc.sync, vs_plane, vs_scales, (0, 1, 2, 3))
        idx6 = load_list(offs6, "idx6")

        short = [new_tile([P, I], F32, f"short{t}") for t in range(PACK)]
        level = [new_tile([P, PACK, P], F32, f"level{h}") for h in range(HALVES)]
        cols = P // GROUP

        def shorten(t, scalar_entries):
            cut = scalar_entries // GROUP
            gather_f32(True, short[t][:, :scalar_entries], tbs[t], idx3[:, :cut])
            gather_f32(False, short[t][:, scalar_entries:], tbs[t], idx3[:, cut:])

        def look_up(t, h, on_scalar):
            gather_f32(on_scalar, level[h][:, t, :], short[t], idx4[:, h * cols : (h + 1) * cols])

        shorten(0, I // 2)
        xt_g = gather_packed(xt_w, idx, U16, "xt_g")
        xt_gs = gather_packed(xt_plane, idx, U8, "xt_gs")
        look_up(0, 0, True)
        look_up(0, 1, True)
        gather_f32(True, short[1][:], tbs[1], idx3[:])
        look_up(1, 0, True)
        look_up(1, 1, True)
        xo_g = gather_packed(xo_w, idx2, U32, "xo_g")
        xo_gs = gather_packed(xo_plane, idx2, U8, "xo_gs")
        shorten(2, I // 2)
        look_up(2, 0, False)
        look_up(2, 1, True)

        a_slot = [psum.tile([P, R], F32, name=f"a_slot{h}") for h in range(HALVES)]
        a_row = [psum.tile([P, PACK, P], F32, name=f"a_row{h}") for h in range(HALVES)]
        def notes_pass(h, first):
            js = slice(h * P, (h + 1) * P)
            nc.tensor.matmul_mx(out=a_slot[h][:], lhsT=xo_g[:, js].bitcast(E4M3X4), lhsT_scale=xo_gs[:, js],
                                rhs=w0_w[:].bitcast(E2M1X4), rhs_scale=w0_plane[:], start=first, stop=not first)

        def tokens_pass(h, first):
            js = slice(h * P, (h + 1) * P)
            nc.tensor.matmul_mx(out=a_slot[h][:], lhsT=xt_g[:, js].bitcast(E2M1X4), lhsT_scale=xt_gs[:, js],
                                rhs=w_w[:].bitcast(E4M3X4), rhs_scale=w_plane[:], start=first, stop=not first)

        notes_pass(0, True)
        tokens_pass(0, False)
        tokens_pass(1, True)
        notes_pass(1, False)

        def turn(h, name):
            dealt = new_tile([P, PACK, P], F32, name)
            nc.scalar.copy(dealt[:], a_slot[h][:].rearrange("j (m t) -> j t m", t=PACK))
            for t in range(PACK):
                nc.tensor.transpose(a_row[h][:, t, :], dealt[:, t, :], identity[:])

        turn(0, "dealt")
        shorten(3, I // 2)
        look_up(3, 0, True)
        turn(1, "tb3")
        look_up(3, 1, True)
        vs_g = gather_packed(vs_w, idx5, U16, "vs_g")
        vs_gs = gather_packed(vs_plane, idx5, U8, "vs_gs")

        def larger(h):
            hid = new_tile([P, P, PACK], BF16, "vs_plane")
            nc.vector.tensor_tensor(hid[:].rearrange("p (c i) t -> p c t i", i=PACK),
                                    a_row[h][:].rearrange("p t (c i) -> p c t i", i=PACK),
                                    level[h][:].rearrange("p t (c i) -> p c t i", i=PACK), MAX)
            return hid

        def quantise(h, hid):
            codes = new_tile([P, P], U32, f"codes{h}")
            scales = new_tile([P, P], U8, f"scales{h}")
            nc.vector.quantize_mx(out=codes[:].bitcast(E5M2X4), scales=scales[:],
                                  in_=hid[:].rearrange("p j t -> p (j t)"))
            return codes, scales

        def multiply(dst, u, codes, scales):
            ns = slice(u * P, (u + 1) * P)
            nc.tensor.matmul_mx(out=dst, lhsT=vs_g[:, ns].bitcast(E2M1X4), lhsT_scale=vs_gs[:, ns],
                                rhs=codes[:].bitcast(E5M2X4), rhs_scale=scales[:], start=True, stop=True)

        def page_columns(u, h):
            return pages[u][:].indirect(idx6[:, h * cols : (h + 1) * cols])

        banks = [[psum.tile([P, P], F32, name=f"bank{h}{u}") for u in range(N // P)] for h in range(HALVES)]
        results = [[new_tile([P, P], F32, f"result{h}{u}") for u in range(N // P)] for h in range(HALVES)]

        def products(h, hid):
            codes, scales = quantise(h, hid)
            for u in range(N // P):
                multiply(banks[h][u][:], u, codes, scales)
            nc.scalar.copy(results[h][0][:], banks[h][0][:])
            nc.scalar.activation(page_columns(0, h), results[h][0][:], COPY)
            return codes

        codes = products(0, larger(0))
        hid = larger(1)
        nc.vector.tensor_copy(results[0][1][:], banks[0][1][:])
        products(1, hid)
        nc.vector.tensor_copy(page_columns(1, 0), results[0][1][:])
        nc.vector.tensor_copy(results[1][1][:], banks[1][1][:])
        nc.vector.tensor_copy(page_columns(1, 1), results[1][1][:])
        nc.scalar.dma_start(out=out[:P, :], in_=pages[0][:])
        nc.sync.dma_start(out=out[P:, :], in_=pages[1][:])
